import numpy as np
import ml_dtypes


def mxq(x, axis, fmt="e4m3"):
    dtype, down = {"e4m3": (ml_dtypes.float8_e4m3fn, 7), "e5m2": (ml_dtypes.float8_e5m2, 14)}[fmt]
    v = np.moveaxis(np.asarray(x, np.float32).astype(ml_dtypes.bfloat16).astype(np.float64), axis, -1)
    blocks = v.reshape(v.shape[:-1] + (-1, 32))
    amax = np.abs(blocks).max(-1, keepdims=True)
    byte = np.maximum(np.where(amax > 0, np.frexp(amax)[1] - 1 + 127, 0) - down, 1)
    scale = np.exp2(byte - 127.0)
    codes = (blocks / scale).astype(np.float32).astype(dtype).astype(np.float64)
    return np.moveaxis((codes * scale).reshape(v.shape), -1, axis)


WIDE = False


def mx_kscale(k):
    if not WIDE:
        return np.ones(k)
    levels = np.array([10, -10, 5, -5, 0])
    if k % 512:
        return np.exp2(np.random.permutation(np.resize(levels, k // 32))).repeat(32)
    a = np.empty((k // 512, 16))
    for p in range(k // 512):
        a[p, :8] = np.random.permutation(np.resize(levels, 8))
        for g in range(8):
            far = levels[np.abs(levels - a[p, g]) >= 10]
            a[p, g + 8] = far[np.random.randint(len(far))]
    return np.exp2(a.ravel()).repeat(32)


def f64(x):
    return np.asarray(x).astype(np.float64)


def striped(idx):
    return np.tile(np.asarray(idx).reshape(-1, 16).T, (8, 1)).astype(np.uint16)


def unstriped(offs):
    return offs[:16].T.reshape(-1).astype(np.int64)


def striped8(idx):
    return np.asarray(idx).reshape(8, -1, 16).transpose(0, 2, 1).reshape(128, -1).astype(np.uint16)


def unstriped8(offs):
    return offs.reshape(8, 16, -1).transpose(0, 2, 1).reshape(8, -1).astype(np.int64)


def pick8(x, idx, run):
    r = np.arange(len(x))
    return x[r[:, None], idx[r % (8 * run) // run]]


E2M1 = np.array([0.0, 0.5, 1.0, 1.5, 2.0, 3.0, 4.0, 6.0, -0.0, -0.5, -1.0, -1.5, -2.0, -3.0, -4.0, -6.0])


def pack_weight(w, fmt):
    k, n = w.shape
    w = f64(np.asarray(w, np.float32).astype(ml_dtypes.bfloat16)).reshape(k // 32, 32, n)
    amax = np.abs(w).max(1)
    if fmt == "e4m3":
        byte = np.frexp(amax)[1] - 1 + 127 - 7
    else:
        mant, ex = np.frexp(amax / 6.0)
        byte = np.where(mant > 0.5, ex, ex - 1) + 127
    byte = np.clip(np.where(amax > 0, byte, 1), 1, 254)
    scaled = (w * np.exp2(127.0 - byte)[:, None, :]).reshape(k, n).astype(np.float32)
    by_word = np.ascontiguousarray(scaled.reshape(k // 512, 128, 4, n).transpose(0, 1, 3, 2))
    if fmt == "e4m3":
        words = by_word.astype(ml_dtypes.float8_e4m3fn).view(np.uint8)
    else:
        c = by_word.astype(ml_dtypes.float4_e2m1fn).view(np.uint8) & 0xF
        words = (c[..., 0::2] | (c[..., 1::2] << 4)).reshape(k // 512, 128, 2 * n)
    return np.ascontiguousarray(words), np.ascontiguousarray(byte.astype(np.uint8).reshape(k // 512, 16, n))


def unpack_weight(words, scales, fmt):
    g, _, n = scales.shape
    words = np.ascontiguousarray(words).reshape(g, 128, n, -1)
    if fmt == "e4m3":
        vals = words.view(ml_dtypes.float8_e4m3fn).astype(np.float64)
    else:
        nib = np.empty((g, 128, n, 4), np.uint8)
        nib[..., 0::2] = words & 0xF
        nib[..., 1::2] = words >> 4
        vals = E2M1[nib]
    vals = vals * np.repeat(np.exp2(scales.astype(np.float64) - 127.0), 8, axis=1)[..., None]
    return vals.transpose(0, 1, 3, 2).reshape(g * 512, n)


K, J, R, T, Z, M, C, O, S, N, V = 512, 256, 512, 1024, 512, 1024, 512, 128, 128, 256, 1024


def setup_inputs():
    n = np.random.standard_normal
    idx = np.random.permutation(T)[:J]
    idx2 = np.random.permutation(M)[:J]
    idx3 = np.stack([np.random.permutation(C)[:J] for _ in range(8)])
    idx4 = np.stack([np.random.permutation(C)[:S] for _ in range(8)])
    idx5 = np.stack([np.random.permutation(C)[:S] for _ in range(8)])
    idx6 = np.stack([np.random.permutation(C)[:O] for _ in range(8)])
    idx7 = np.random.permutation(V)[:N]
    fk = mx_kscale(K)
    fr = mx_kscale(R)
    fz = mx_kscale(Z)
    xtp = pack_weight(n((K, T)) * fk[:, None], "e2m1")
    wp = pack_weight(n((K, R)) * 1 / np.sqrt(K) / fk[:, None] * fr, "e4m3")
    xop = pack_weight(n((Z, M)) / fz[:, None], "e4m3")
    w2p = pack_weight(n((Z, R)) * 1 / np.sqrt(Z) * fz[:, None] * fr, "e2m1")
    vsp = pack_weight(n((R, V)) * 1 / np.sqrt(R) / fr[:, None], "e2m1")
    return {
        "xt_words": xtp[0],
        "xt_scales": xtp[1],
        "w_words": wp[0],
        "w_scales": wp[1],
        "xo_words": xop[0],
        "xo_scales": xop[1],
        "w2_words": w2p[0],
        "w2_scales": w2p[1],
        "sa": (np.random.uniform(0.5, 1.6, (R, 1))).astype(np.float32),
        "sb": (np.random.uniform(0.5, 1.6, (R, 1))).astype(np.float32),
        "vs_words": vsp[0],
        "vs_scales": vsp[1],
        "offs": striped(idx),
        "offs2": striped(idx2),
        "offs3": striped8(idx3),
        "offs4": striped8(idx4),
        "offs5": striped8(idx5),
        "offs6": striped8(idx6),
        "offs7": striped(idx7),
    }


def reference(xt_words, xt_scales, w_words, w_scales, xo_words, xo_scales, w2_words, w2_scales, sa, sb, vs_words, vs_scales, offs, offs2, offs3, offs4, offs5, offs6, offs7):
    idx = unstriped(offs)
    idx2 = unstriped(offs2)
    idx3 = unstriped8(offs3)
    idx4 = unstriped8(offs4)
    idx5 = unstriped8(offs5)
    idx6 = unstriped8(offs6)
    idx7 = unstriped(offs7)
    xtu = unpack_weight(xt_words, xt_scales, "e2m1")
    wu = unpack_weight(w_words, w_scales, "e4m3")
    xou = unpack_weight(xo_words, xo_scales, "e4m3")
    w2u = unpack_weight(w2_words, w2_scales, "e2m1")
    vsu = unpack_weight(vs_words, vs_scales, "e2m1")
    xtidxg = xtu[:, idx]
    xoidx2g = xou[:, idx2]
    a = wu.T @ xtidxg + w2u.T @ xoidx2g
    pw = np.zeros((R, C))
    pw[np.arange(R)[:, None], idx3[np.arange(R) % 512 // 64]] = a
    h1 = pick8(pw, idx4, 64) * f64(sa)
    pv = np.zeros((R, C))
    pv[np.arange(R)[:, None], idx5[np.arange(R) % 512 // 64]] = h1
    pg = pw + pv
    hid = pick8(pg, idx6, 64) * f64(sb)
    vsidx7g = vsu[:, idx7]
    hidq = mxq(hid, 0, "e4m3")
    y = vsidx7g.T @ hidq
    return y

@@ -1,0 +1,192 @@
+from contextlib import ExitStack
+
+import concourse.mybir as mybir
+
+F32 = mybir.dt.float32
+BF16 = mybir.dt.bfloat16
+I32 = mybir.dt.int32
+U32 = mybir.dt.uint32
+U16 = mybir.dt.uint16
+U8 = mybir.dt.uint8
+FP8X4 = mybir.dt.float8_e4m3fn_x4
+FP4X4 = mybir.dt.float4_e2m1fn_x4
+COPY = mybir.ActivationFunctionType.Copy
+ADD = mybir.AluOpType.add
+
+P = 128
+PACK = 4
+J, R, T, C, O, S, N, V = 256, 512, 1024, 512, 128, 128, 256, 1024
+H = J // 2
+FLOPS = 2 * (512 * R * J + 512 * R * J + R * N * O)
+
+
+def tile_picked_tokens_plain_bank_echo_store_plain_kernel(
+    tc, xt_words, xt_scales, w_words, w_scales, xo_words, xo_scales, w2_words, w2_scales,
+    sa, sb, vs_words, vs_scales, offs, offs2, offs3, offs4, offs5, offs6, offs7, out,
+):
+    nc = tc.nc
+    with ExitStack() as ctx:
+        lists = ctx.enter_context(tc.tile_pool(name="lists", bufs=1))
+        sbuf = ctx.enter_context(tc.tile_pool(name="sbuf", bufs=1))
+        psum = ctx.enter_context(tc.psum_pool(name="psum", bufs=1))
+
+        def held(shape, dtype, name, tag=None):
+            return sbuf.tile(shape, dtype, name=name, tag=tag or name, align_bytes=64)
+
+        def list_tile(src, name):
+            return lists.tile(list(src.shape), U16, name=name)
+
+        def load_rows(queue, window, scales, q):
+            queue.dma_start(out=window[32 * q : 32 * q + 4, :].bitcast(I32), in_=scales[0, 4 * q : 4 * q + 4, :].bitcast(I32))
+
+        l1, l2, l3, l4, l5, l6, l7 = [
+            list_tile(src, "list%d" % i) for i, src in enumerate((offs, offs2, offs3, offs4, offs5, offs6, offs7))
+        ]
+        xt_w = held([P, T], U16, "xt_w")
+        xt_s = held([P, T], U8, "xt_s")
+        xo_w = held([P, T], U32, "xo_w")
+        xo_s = held([P, T], U8, "xo_s")
+        vs_w = held([P, V], U16, "vs_w")
+        vs_s = held([P, V], U8, "vs_s")
+        w_raw = held([P, R], U32, "w_raw")
+        w2_raw = held([P, R], U16, "w2_raw")
+        stage = held([4, 4, 2, R // 4], I32, "stage")
+        spread = held([P, 2 * R // 4], I32, "spread")
+        sa_t = held([P, PACK], F32, "sa_t")
+        sb_t = held([P, PACK], F32, "sb_t")
+        pw = [held([P, C], F32, "pw%d" % t) for t in range(PACK)]
+
+        for win in (xt_s, xo_s):
+            nc.vector.memset(win[:].bitcast(I32), 0)
+        nc.vector.memset(spread[:], 0)
+        for t in range(PACK):
+            nc.vector.memset(pw[t][:], 0.0)
+        nc.vector.memset(vs_s[:].bitcast(I32), 0)
+
+        nc.sync.dma_start(l1[:], offs)
+        for m, scales in enumerate((w_scales, w2_scales)):
+            nc.scalar.dma_start(out=stage[:, :, m, :], in_=scales[0].bitcast(I32).rearrange("(q i) c -> i q c", i=4))
+        nc.sync.dma_start(out=w_raw[:].bitcast(I32), in_=w_words[0].rearrange("p n t -> p (n t)").bitcast(I32))
+        nc.sync.dma_start(out=w2_raw[:].bitcast(I32), in_=w2_words[0].bitcast(I32))
+        nc.sync.dma_start(out=xt_w[:].bitcast(I32), in_=xt_words[0].bitcast(I32))
+        for q in range(4):
+            load_rows(nc.scalar, xt_s, xt_scales, q)
+        nc.sync.dma_start(l2[:], offs2)
+        nc.sync.dma_start(out=xo_w[:].bitcast(I32), in_=xo_words[0].rearrange("p n t -> p (n t)").bitcast(I32))
+        for q in range(4):
+            load_rows(nc.scalar if q < 2 else nc.sync, xo_s, xo_scales, q)
+        nc.sync.dma_start(l3[:], offs3)
+        nc.sync.dma_start(l4[:], offs4)
+        nc.sync.dma_start(out=sa_t[:], in_=sa.rearrange("(p t) o -> p (t o)", t=PACK))
+        nc.sync.dma_start(l5[:], offs5)
+        nc.sync.dma_start(l7[:], offs7)
+        nc.sync.dma_start(out=vs_w[:].bitcast(I32), in_=vs_words[0].bitcast(I32))
+        for q in range(4):
+            load_rows(nc.sync, vs_s, vs_scales, q)
+        nc.sync.dma_start(l6[:], offs6)
+        nc.sync.dma_start(out=sb_t[:], in_=sb.rearrange("(p t) o -> p (t o)", t=PACK))
+
+        w_d = held([P, PACK, P], U32, "w_d")
+        w2_d = held([P, PACK, P], U16, "w2_d")
+        nc.scalar.copy(out=w_d[:], in_=w_raw[:].rearrange("p (m t) -> p t m", t=PACK))
+        nc.scalar.copy(out=w2_d[:], in_=w2_raw[:].rearrange("p (m t) -> p t m", t=PACK))
+
+        for q in range(4):
+            nc.vector.tensor_copy(out=spread[32 * q : 32 * q + 4, :], in_=stage[:, q, :, :].rearrange("p m c -> p (m c)"))
+        by_tile = spread[:].bitcast(U8).rearrange("p (c t) -> p t c", t=PACK)
+        s_first = held([P, 2 * P], U8, "s_first")
+        s_rest = held([P, PACK - 1, 2 * P], U8, "s_rest")
+        nc.vector.tensor_copy(out=s_first[:], in_=by_tile[:, 0, :])
+        s_d = [s_first[:]] + [s_rest[:, t, :] for t in range(PACK - 1)]
+
+        xg_w = [held([P, H], U16, "xg_w%d" % h) for h in range(2)]
+        xg_s = [held([P, H], U8, "xg_s%d" % h) for h in range(2)]
+        og_w = [held([P, H], U32, "og_w%d" % h) for h in range(2)]
+        og_s = [held([P, H], U8, "og_s%d" % h) for h in range(2)]
+
+        def gather_half(h):
+            cols = slice(h * H // 16, (h + 1) * H // 16)
+            nc.vector.tensor_copy(out=xg_w[h][:], in_=xt_w[:].indirect(l1[:, cols]))
+            nc.vector.tensor_copy(out=xg_s[h][:], in_=xt_s[:].indirect(l1[:, cols]))
+            nc.vector.tensor_copy(out=og_s[h][:], in_=xo_s[:].indirect(l2[:, cols]))
+            nc.vector.tensor_copy(out=og_w[h][:], in_=xo_w[:].indirect(l2[:, cols]))
+
+        def product(acc, t, h):
+            nc.tensor.matmul_mx(out=acc, lhsT=w_d[:, t, :].bitcast(FP8X4), lhsT_scale=s_d[t][:, 0:P],
+                                rhs=xg_w[h][:].bitcast(FP4X4), rhs_scale=xg_s[h][:], start=True, stop=False)
+            nc.tensor.matmul_mx(out=acc, lhsT=w2_d[:, t, :].bitcast(FP4X4), lhsT_scale=s_d[t][:, P : 2 * P],
+                                rhs=og_w[h][:].bitcast(FP8X4), rhs_scale=og_s[h][:], start=False, stop=True)
+
+        gather_half(0)
+        nc.vector.tensor_copy(out=s_rest[:], in_=by_tile[:, 1:PACK, :])
+        a0 = [held([P, H], F32, "a0_%d" % t) for t in range(PACK)]
+        for t in range(PACK):
+            acc = psum.tile([P, H], F32, name="acc0_%d" % t)
+            product(acc[:], t, 0)
+            if t == 0:
+                nc.scalar.activation(out=a0[t][:], in_=acc[:], func=COPY)
+            else:
+                nc.vector.tensor_copy(out=a0[t][:], in_=acc[:])
+        gather_half(1)
+        a1 = [held([P, 2, H], F32, "a1_%d" % u) for u in range(2)]
+        for u in range(2):
+            acc = psum.tile([P, 2, H], F32, name="acc1_%d" % u)
+            for i in range(2):
+                product(acc[:, i, :], 2 * u + i, 1)
+            nc.vector.tensor_copy(out=a1[u][:], in_=acc[:])
+
+        pv = [held([P, C], F32, "pv%d" % t, tag=tag) for t, tag in enumerate(("xt_w", "xt_s", "xo_s", "xo_w"))]
+        for t in range(PACK):
+            nc.vector.memset(pv[t][:], 0.0)
+        h1 = [held([P, S], F32, "h1_%d" % t) for t in range(PACK)]
+        pg = [held([P, C], F32, "pg%d" % t) for t in range(PACK)]
+
+        def put_a(t, h):
+            src = a0[t][:] if h == 0 else a1[t // 2][:, t % 2, :]
+            nc.scalar.activation(out=pw[t][:].indirect(l3[:, h * H // 16 : (h + 1) * H // 16]), in_=src, func=COPY)
+
+        def take(t):
+            nc.scalar.activation(out=h1[t][:], in_=pw[t][:].indirect(l4[:]), func=COPY, scale=sa_t[:, t : t + 1])
+
+        def put_echo(t):
+            nc.scalar.activation(out=pv[t][:].indirect(l5[:]), in_=h1[t][:], func=COPY)
+            nc.vector.tensor_tensor(out=pg[t][:], in0=pw[t][:], in1=pv[t][:], op=ADD)
+
+        for t in range(PACK):
+            put_a(t, 0)
+        put_a(0, 1)
+        vg_w = held([P, N], U16, "vg_w")
+        vg_s = held([P, N], U8, "vg_s")
+        nc.vector.tensor_copy(out=vg_w[:], in_=vs_w[:].indirect(l7[:]))
+        nc.vector.tensor_copy(out=vg_s[:], in_=vs_s[:].indirect(l7[:]))
+        for step in range(1, PACK + 2):
+            if step < PACK:
+                put_a(step, 1)
+            if step <= PACK:
+                take(step - 1)
+            if step >= 2:
+                put_echo(step - 2)
+
+        hid = held([P, PACK, O], BF16, "hid", tag="h1_2")
+        for t in range(PACK):
+            nc.scalar.activation(out=hid[:, t, :], in_=pg[t][:].indirect(l6[:]), func=COPY, scale=sb_t[:, t : t + 1])
+
+        woven = [held([P, O // 2, PACK], BF16, "woven%d" % u) for u in range(2)]
+        hq_w = held([P, O], U32, "hq_w")
+        hq_s = held([P, O], U8, "hq_s")
+        for u in range(2):
+            nc.vector.tensor_copy(out=woven[u][:], in_=hid[:, :, u * 64 : (u + 1) * 64].rearrange("p t o -> p o t"))
+        for u in range(2):
+            nc.vector.quantize_mx(out=hq_w[:, u * 64 : (u + 1) * 64].bitcast(FP8X4), scales=hq_s[:, u * 64 : (u + 1) * 64],
+                                  in_=woven[u][:].rearrange("p o t -> p (o t)"))
+        for u in range(2):
+            y = psum.tile([P, O], F32, name="y%d" % u)
+            nc.tensor.matmul_mx(out=y[:], lhsT=vg_w[:, u * P : (u + 1) * P].bitcast(FP4X4), lhsT_scale=vg_s[:, u * P : (u + 1) * P],
+                                rhs=hq_w[:].bitcast(FP8X4), rhs_scale=hq_s[:], start=True, stop=True)
+            res = held([P, O], F32, "res%d" % u)
+            if u == 0:
+                nc.vector.tensor_copy(out=res[:], in_=y[:])
+                nc.sync.dma_start(out=out[u * P : (u + 1) * P, :], in_=res[:])
+            else:
+                nc.scalar.activation(out=res[:], in_=y[:], func=COPY)
+                nc.scalar.dma_start(out=out[u * P : (u + 1) * P, :], in_=res[:])

@@ -17,6 +17,7 @@ P = 128
 PACK = 4
 J, R, T, C, O, S, N, V = 256, 512, 1024, 512, 128, 128, 256, 1024
 H = J // 2
+SPLIT = 2
 FLOPS = 2 * (512 * R * J + 512 * R * J + R * N * O)
 
 
@@ -28,6 +29,7 @@ def tile_picked_tokens_plain_bank_echo_store_plain_kernel(
     with ExitStack() as ctx:
         lists = ctx.enter_context(tc.tile_pool(name="lists", bufs=1))
         sbuf = ctx.enter_context(tc.tile_pool(name="sbuf", bufs=1))
+        reused = ctx.enter_context(tc.tile_pool(name="reused", bufs=1))
         psum = ctx.enter_context(tc.psum_pool(name="psum", bufs=1))
 
         def held(shape, dtype, name, tag=None):
@@ -47,62 +49,57 @@ def tile_picked_tokens_plain_bank_echo_store_plain_kernel(
         xo_w = held([P, T], U32, "xo_w")
         xo_s = held([P, T], U8, "xo_s")
         vs_w = held([P, V], U16, "vs_w")
-        vs_s = held([P, V], U8, "vs_s")
         w_raw = held([P, R], U32, "w_raw")
-        w2_raw = held([P, R], U16, "w2_raw")
-        stage = held([4, 4, 2, R // 4], I32, "stage")
-        spread = held([P, 2 * R // 4], I32, "spread")
+        w2_raw = reused.tile([P, R], U16, name="w2_raw", offset=0, align_bytes=64)
+        xt_stage = held([4, 4, T // 4], I32, "xt_stage")
+        w_stage = held([4, 2, 4, R // 4], I32, "w_stage")
+        spread = held([P, 2, R // 4], I32, "spread")
         sa_t = held([P, PACK], F32, "sa_t")
         sb_t = held([P, PACK], F32, "sb_t")
         pw = [held([P, C], F32, "pw%d" % t) for t in range(PACK)]
 
-        for win in (xt_s, xo_s):
+        for win in (xo_s, xt_s):
             nc.vector.memset(win[:].bitcast(I32), 0)
         nc.vector.memset(spread[:], 0)
         for t in range(PACK):
-            nc.vector.memset(pw[t][:], 0.0)
-        nc.vector.memset(vs_s[:].bitcast(I32), 0)
+            (nc.vector if t < 2 else nc.gpsimd).memset(pw[t][:], 0.0)
 
+        for stage, scales in ((xt_stage[:], xt_scales), (w_stage[:, 0], w_scales), (w_stage[:, 1], w2_scales)):
+            nc.sync.dma_start(out=stage, in_=scales[0].bitcast(I32).rearrange("(q i) c -> i q c", i=4))
         nc.sync.dma_start(l1[:], offs)
-        for m, scales in enumerate((w_scales, w2_scales)):
-            nc.scalar.dma_start(out=stage[:, :, m, :], in_=scales[0].bitcast(I32).rearrange("(q i) c -> i q c", i=4))
-        nc.sync.dma_start(out=w_raw[:].bitcast(I32), in_=w_words[0].rearrange("p n t -> p (n t)").bitcast(I32))
-        nc.sync.dma_start(out=w2_raw[:].bitcast(I32), in_=w2_words[0].bitcast(I32))
-        nc.sync.dma_start(out=xt_w[:].bitcast(I32), in_=xt_words[0].bitcast(I32))
-        for q in range(4):
-            load_rows(nc.scalar, xt_s, xt_scales, q)
         nc.sync.dma_start(l2[:], offs2)
+        nc.sync.dma_start(out=w_raw[:].bitcast(I32), in_=w_words[0].rearrange("p n t -> p (n t)").bitcast(I32))
+        nc.sync.dma_start(out=xt_w[:].bitcast(I32), in_=xt_words[0].bitcast(I32))
         nc.sync.dma_start(out=xo_w[:].bitcast(I32), in_=xo_words[0].rearrange("p n t -> p (n t)").bitcast(I32))
         for q in range(4):
-            load_rows(nc.scalar if q < 2 else nc.sync, xo_s, xo_scales, q)
+            load_rows(nc.sync, xo_s, xo_scales, q)
+        nc.sync.dma_start(out=w2_raw[:].bitcast(I32), in_=w2_words[0].bitcast(I32))
         nc.sync.dma_start(l3[:], offs3)
         nc.sync.dma_start(l4[:], offs4)
         nc.sync.dma_start(out=sa_t[:], in_=sa.rearrange("(p t) o -> p (t o)", t=PACK))
         nc.sync.dma_start(l5[:], offs5)
         nc.sync.dma_start(l7[:], offs7)
         nc.sync.dma_start(out=vs_w[:].bitcast(I32), in_=vs_words[0].bitcast(I32))
-        for q in range(4):
-            load_rows(nc.sync, vs_s, vs_scales, q)
         nc.sync.dma_start(l6[:], offs6)
         nc.sync.dma_start(out=sb_t[:], in_=sb.rearrange("(p t) o -> p (t o)", t=PACK))
 
         w_d = held([P, PACK, P], U32, "w_d")
         w2_d = held([P, PACK, P], U16, "w2_d")
-        nc.scalar.copy(out=w_d[:], in_=w_raw[:].rearrange("p (m t) -> p t m", t=PACK))
-        nc.scalar.copy(out=w2_d[:], in_=w2_raw[:].rearrange("p (m t) -> p t m", t=PACK))
+        nc.scalar.copy(out=w_d[:].rearrange("p t m -> p m t"), in_=w_raw[:].rearrange("p (m t) -> p m t", t=PACK))
+        nc.scalar.copy(out=w2_d[:].rearrange("p t m -> p m t"), in_=w2_raw[:].rearrange("p (m t) -> p m t", t=PACK))
 
         for q in range(4):
-            nc.vector.tensor_copy(out=spread[32 * q : 32 * q + 4, :], in_=stage[:, q, :, :].rearrange("p m c -> p (m c)"))
-        by_tile = spread[:].bitcast(U8).rearrange("p (c t) -> p t c", t=PACK)
-        s_first = held([P, 2 * P], U8, "s_first")
-        s_rest = held([P, PACK - 1, 2 * P], U8, "s_rest")
-        nc.vector.tensor_copy(out=s_first[:], in_=by_tile[:, 0, :])
-        s_d = [s_first[:]] + [s_rest[:, t, :] for t in range(PACK - 1)]
+            nc.vector.tensor_copy(out=xt_s[32 * q : 32 * q + 4, :].bitcast(I32), in_=xt_stage[:, q, :])
+            nc.vector.tensor_copy(out=spread[32 * q : 32 * q + 4], in_=w_stage[:, :, q, :])
+        s_all = held([P, PACK, 2 * P], U8, "s_all")
+        by_column = spread[:].rearrange("p m c -> p (m c)").bitcast(U8).rearrange("p (c t) -> p c t", t=PACK)
+        nc.vector.tensor_copy(out=s_all[:].rearrange("p t c -> p c t"), in_=by_column)
+        s_d = [s_all[:, t, :] for t in range(PACK)]
 
-        xg_w = [held([P, H], U16, "xg_w%d" % h) for h in range(2)]
-        xg_s = [held([P, H], U8, "xg_s%d" % h) for h in range(2)]
-        og_w = [held([P, H], U32, "og_w%d" % h) for h in range(2)]
-        og_s = [held([P, H], U8, "og_s%d" % h) for h in range(2)]
+        xg_w = [held([P, H], U16, "xg_w0"), reused.tile([P, H], U16, name="xg_w1", offset=0, align_bytes=64)]
+        xg_s = [held([P, H], U8, "xg_s0"), reused.tile([P, H], U8, name="xg_s1", offset=2 * H, align_bytes=64)]
+        og_s = [held([P, H], U8, "og_s0"), reused.tile([P, H], U8, name="og_s1", offset=3 * H, align_bytes=64)]
+        og_w = [held([P, H], U32, "og_w0"), reused.tile([P, H], U32, name="og_w1", offset=4 * H, align_bytes=64)]
 
         def gather_half(h):
             cols = slice(h * H // 16, (h + 1) * H // 16)
@@ -118,32 +115,34 @@ def tile_picked_tokens_plain_bank_echo_store_plain_kernel(
                                 rhs=og_w[h][:].bitcast(FP8X4), rhs_scale=og_s[h][:], start=False, stop=True)
 
         gather_half(0)
-        nc.vector.tensor_copy(out=s_rest[:], in_=by_tile[:, 1:PACK, :])
-        a0 = [held([P, H], F32, "a0_%d" % t) for t in range(PACK)]
-        for t in range(PACK):
-            acc = psum.tile([P, H], F32, name="acc0_%d" % t)
+        early = [held([P, H], F32, "early%d" % t) for t in range(SPLIT)]
+        for t in range(SPLIT):
+            acc = psum.tile([P, H], F32, name="acc_early%d" % t)
             product(acc[:], t, 0)
             if t == 0:
-                nc.scalar.activation(out=a0[t][:], in_=acc[:], func=COPY)
+                nc.scalar.activation(out=early[t][:], in_=acc[:], func=COPY)
             else:
-                nc.vector.tensor_copy(out=a0[t][:], in_=acc[:])
+                nc.vector.tensor_copy(out=early[t][:], in_=acc[:])
         gather_half(1)
-        a1 = [held([P, 2, H], F32, "a1_%d" % u) for u in range(2)]
-        for u in range(2):
-            acc = psum.tile([P, 2, H], F32, name="acc1_%d" % u)
-            for i in range(2):
-                product(acc[:, i, :], 2 * u + i, 1)
-            nc.vector.tensor_copy(out=a1[u][:], in_=acc[:])
+        late = held([P, SPLIT, H], F32, "late")
+        acc = psum.tile([P, SPLIT, H], F32, name="acc_late")
+        for t in range(SPLIT):
+            product(acc[:, t, :], t, 1)
+        nc.vector.tensor_copy(out=late[:], in_=acc[:])
+        whole = [held([P, J], F32, "whole%d" % t) for t in range(SPLIT, PACK)]
+        for t in range(SPLIT, PACK):
+            acc = psum.tile([P, 2, H], F32, name="acc_whole%d" % t)
+            for h in range(2):
+                product(acc[:, h, :], t, h)
+            nc.vector.tensor_copy(out=whole[t - SPLIT][:], in_=acc[:].rearrange("p h j -> p (h j)"))
 
         pv = [held([P, C], F32, "pv%d" % t, tag=tag) for t, tag in enumerate(("xt_w", "xt_s", "xo_s", "xo_w"))]
         for t in range(PACK):
             nc.vector.memset(pv[t][:], 0.0)
         h1 = [held([P, S], F32, "h1_%d" % t) for t in range(PACK)]
-        pg = [held([P, C], F32, "pg%d" % t) for t in range(PACK)]
 
-        def put_a(t, h):
-            src = a0[t][:] if h == 0 else a1[t // 2][:, t % 2, :]
-            nc.scalar.activation(out=pw[t][:].indirect(l3[:, h * H // 16 : (h + 1) * H // 16]), in_=src, func=COPY)
+        def put_a(t, src, first, count):
+            nc.scalar.activation(out=pw[t][:].indirect(l3[:, first // 16 : (first + count) // 16]), in_=src, func=COPY)
 
         def take(t):
             nc.scalar.activation(out=h1[t][:], in_=pw[t][:].indirect(l4[:]), func=COPY, scale=sa_t[:, t : t + 1])
@@ -152,20 +151,26 @@ def tile_picked_tokens_plain_bank_echo_store_plain_kernel(
             nc.scalar.activation(out=pv[t][:].indirect(l5[:]), in_=h1[t][:], func=COPY)
             nc.vector.tensor_tensor(out=pg[t][:], in0=pw[t][:], in1=pv[t][:], op=ADD)
 
-        for t in range(PACK):
-            put_a(t, 0)
-        put_a(0, 1)
-        vg_w = held([P, N], U16, "vg_w")
+        for t in range(SPLIT):
+            put_a(t, early[t][:], 0, H)
+        for t in range(SPLIT):
+            put_a(t, late[:, t, :], H, H)
+        for t in range(SPLIT, PACK):
+            put_a(t, whole[t - SPLIT][:], 0, J)
+
+        vs_s = held([P, V], U8, "vs_s", tag="early0")
+        nc.vector.memset(vs_s[:].bitcast(I32), 0)
+        for q in range(4):
+            load_rows(nc.sync, vs_s, vs_scales, q)
+        vg_w = held([P, N], U16, "vg_w", tag="late")
         vg_s = held([P, N], U8, "vg_s")
-        nc.vector.tensor_copy(out=vg_w[:], in_=vs_w[:].indirect(l7[:]))
         nc.vector.tensor_copy(out=vg_s[:], in_=vs_s[:].indirect(l7[:]))
-        for step in range(1, PACK + 2):
-            if step < PACK:
-                put_a(step, 1)
-            if step <= PACK:
-                take(step - 1)
-            if step >= 2:
-                put_echo(step - 2)
+        nc.vector.tensor_copy(out=vg_w[:], in_=vs_w[:].indirect(l7[:]))
+        pg = [held([P, C], F32, "pg%d" % t, tag={0: "vs_w", 1: "early0"}.get(t)) for t in range(PACK)]
+        for t in range(PACK):
+            take(t)
+        for t in range(PACK):
+            put_echo(t)
 
         hid = held([P, PACK, O], BF16, "hid", tag="h1_2")
         for t in range(PACK):

@@ -17,7 +17,7 @@ P = 128
 PACK = 4
 J, R, T, C, O, S, N, V = 256, 512, 1024, 512, 128, 128, 256, 1024
 H = J // 2
-SPLIT = 2
+SPLIT = 3
 FLOPS = 2 * (512 * R * J + 512 * R * J + R * N * O)
 
 
@@ -30,6 +30,7 @@ def tile_picked_tokens_plain_bank_echo_store_plain_kernel(
         lists = ctx.enter_context(tc.tile_pool(name="lists", bufs=1))
         sbuf = ctx.enter_context(tc.tile_pool(name="sbuf", bufs=1))
         reused = ctx.enter_context(tc.tile_pool(name="reused", bufs=1))
+        sums = ctx.enter_context(tc.tile_pool(name="sums", bufs=1))
         psum = ctx.enter_context(tc.psum_pool(name="psum", bufs=1))
 
         def held(shape, dtype, name, tag=None):
@@ -48,7 +49,8 @@ def tile_picked_tokens_plain_bank_echo_store_plain_kernel(
         xt_s = held([P, T], U8, "xt_s")
         xo_w = held([P, T], U32, "xo_w")
         xo_s = held([P, T], U8, "xo_s")
-        vs_w = held([P, V], U16, "vs_w")
+        vs_w = sums.tile([P, V], U16, name="vs_w", offset=4 * C - V, align_bytes=64)
+        vs_s = sums.tile([P, V], U8, name="vs_s", offset=12 * C - V // 2, align_bytes=64)
         w_raw = held([P, R], U32, "w_raw")
         w2_raw = reused.tile([P, R], U16, name="w2_raw", offset=0, align_bytes=64)
         xt_stage = held([4, 4, T // 4], I32, "xt_stage")
@@ -62,7 +64,8 @@ def tile_picked_tokens_plain_bank_echo_store_plain_kernel(
             nc.vector.memset(win[:].bitcast(I32), 0)
         nc.vector.memset(spread[:], 0)
         for t in range(PACK):
-            (nc.vector if t < 2 else nc.gpsimd).memset(pw[t][:], 0.0)
+            (nc.vector if t < 3 else nc.gpsimd).memset(pw[t][:], 0.0)
+        nc.gpsimd.memset(vs_s[:].bitcast(I32), 0)
 
         for stage, scales in ((xt_stage[:], xt_scales), (w_stage[:, 0], w_scales), (w_stage[:, 1], w2_scales)):
             nc.sync.dma_start(out=stage, in_=scales[0].bitcast(I32).rearrange("(q i) c -> i q c", i=4))
@@ -80,13 +83,19 @@ def tile_picked_tokens_plain_bank_echo_store_plain_kernel(
         nc.sync.dma_start(l5[:], offs5)
         nc.sync.dma_start(l7[:], offs7)
         nc.sync.dma_start(out=vs_w[:].bitcast(I32), in_=vs_words[0].bitcast(I32))
+        for q in range(4):
+            load_rows(nc.sync, vs_s, vs_scales, q)
         nc.sync.dma_start(l6[:], offs6)
         nc.sync.dma_start(out=sb_t[:], in_=sb.rearrange("(p t) o -> p (t o)", t=PACK))
 
         w_d = held([P, PACK, P], U32, "w_d")
-        w2_d = held([P, PACK, P], U16, "w2_d")
+        w2_first = held([P, P], U16, "w2_first")
+        w2_rest = held([P, PACK - 1, P], U16, "w2_rest")
+        w2_d = [w2_first[:]] + [w2_rest[:, t, :] for t in range(PACK - 1)]
         nc.scalar.copy(out=w_d[:].rearrange("p t m -> p m t"), in_=w_raw[:].rearrange("p (m t) -> p m t", t=PACK))
-        nc.scalar.copy(out=w2_d[:].rearrange("p t m -> p m t"), in_=w2_raw[:].rearrange("p (m t) -> p m t", t=PACK))
+        w2_columns = w2_raw[:].rearrange("p (m t) -> p m t", t=PACK)
+        nc.scalar.copy(out=w2_first[:], in_=w2_columns[:, :, 0])
+        nc.scalar.copy(out=w2_rest[:].rearrange("p t m -> p m t"), in_=w2_columns[:, :, 1:PACK])
 
         for q in range(4):
             nc.vector.tensor_copy(out=xt_s[32 * q : 32 * q + 4, :].bitcast(I32), in_=xt_stage[:, q, :])
@@ -111,7 +120,7 @@ def tile_picked_tokens_plain_bank_echo_store_plain_kernel(
         def product(acc, t, h):
             nc.tensor.matmul_mx(out=acc, lhsT=w_d[:, t, :].bitcast(FP8X4), lhsT_scale=s_d[t][:, 0:P],
                                 rhs=xg_w[h][:].bitcast(FP4X4), rhs_scale=xg_s[h][:], start=True, stop=False)
-            nc.tensor.matmul_mx(out=acc, lhsT=w2_d[:, t, :].bitcast(FP4X4), lhsT_scale=s_d[t][:, P : 2 * P],
+            nc.tensor.matmul_mx(out=acc, lhsT=w2_d[t].bitcast(FP4X4), lhsT_scale=s_d[t][:, P : 2 * P],
                                 rhs=og_w[h][:].bitcast(FP8X4), rhs_scale=og_s[h][:], start=False, stop=True)
 
         gather_half(0)
@@ -129,16 +138,16 @@ def tile_picked_tokens_plain_bank_echo_store_plain_kernel(
         for t in range(SPLIT):
             product(acc[:, t, :], t, 1)
         nc.vector.tensor_copy(out=late[:], in_=acc[:])
-        whole = [held([P, J], F32, "whole%d" % t) for t in range(SPLIT, PACK)]
-        for t in range(SPLIT, PACK):
-            acc = psum.tile([P, 2, H], F32, name="acc_whole%d" % t)
-            for h in range(2):
-                product(acc[:, h, :], t, h)
-            nc.vector.tensor_copy(out=whole[t - SPLIT][:], in_=acc[:].rearrange("p h j -> p (h j)"))
+        whole = held([P, PACK - SPLIT, J], F32, "whole")
+        acc = psum.tile([P, PACK - SPLIT, 2, H], F32, name="acc_whole")
+        for h in range(2):
+            for t in range(SPLIT, PACK):
+                product(acc[:, t - SPLIT, h, :], t, h)
+        nc.vector.tensor_copy(out=whole[:].rearrange("p t j -> p (t j)"), in_=acc[:].rearrange("p t h j -> p (t h j)"))
 
         pv = [held([P, C], F32, "pv%d" % t, tag=tag) for t, tag in enumerate(("xt_w", "xt_s", "xo_s", "xo_w"))]
         for t in range(PACK):
-            nc.vector.memset(pv[t][:], 0.0)
+            nc.gpsimd.memset(pv[t][:], 0.0)
         h1 = [held([P, S], F32, "h1_%d" % t) for t in range(PACK)]
 
         def put_a(t, src, first, count):
@@ -156,23 +165,19 @@ def tile_picked_tokens_plain_bank_echo_store_plain_kernel(
         for t in range(SPLIT):
             put_a(t, late[:, t, :], H, H)
         for t in range(SPLIT, PACK):
-            put_a(t, whole[t - SPLIT][:], 0, J)
+            put_a(t, whole[:, t - SPLIT, :], 0, J)
 
-        vs_s = held([P, V], U8, "vs_s", tag="early0")
-        nc.vector.memset(vs_s[:].bitcast(I32), 0)
-        for q in range(4):
-            load_rows(nc.sync, vs_s, vs_scales, q)
-        vg_w = held([P, N], U16, "vg_w", tag="late")
-        vg_s = held([P, N], U8, "vg_s")
+        vg_w = held([P, N], U16, "vg_w", tag="early2")
+        vg_s = held([P, N], U8, "vg_s", tag="late")
         nc.vector.tensor_copy(out=vg_s[:], in_=vs_s[:].indirect(l7[:]))
         nc.vector.tensor_copy(out=vg_w[:], in_=vs_w[:].indirect(l7[:]))
-        pg = [held([P, C], F32, "pg%d" % t, tag={0: "vs_w", 1: "early0"}.get(t)) for t in range(PACK)]
+        pg = [sums.tile([P, C], F32, name="pg%d" % t, offset=4 * C * t, align_bytes=64) for t in range(PACK)]
         for t in range(PACK):
             take(t)
         for t in range(PACK):
             put_echo(t)
 
-        hid = held([P, PACK, O], BF16, "hid", tag="h1_2")
+        hid = held([P, PACK, O], BF16, "hid", tag="h1_3")
         for t in range(PACK):
             nc.scalar.activation(out=hid[:, t, :], in_=pg[t][:].indirect(l6[:]), func=COPY, scale=sb_t[:, t : t + 1])
 

@@ -31,6 +31,7 @@ def tile_picked_tokens_plain_bank_echo_store_plain_kernel(
         sbuf = ctx.enter_context(tc.tile_pool(name="sbuf", bufs=1))
         reused = ctx.enter_context(tc.tile_pool(name="reused", bufs=1))
         sums = ctx.enter_context(tc.tile_pool(name="sums", bufs=1))
+        boards = ctx.enter_context(tc.tile_pool(name="boards", bufs=1))
         psum = ctx.enter_context(tc.psum_pool(name="psum", bufs=1))
 
         def held(shape, dtype, name, tag=None):
@@ -47,7 +48,7 @@ def tile_picked_tokens_plain_bank_echo_store_plain_kernel(
         ]
         xt_w = held([P, T], U16, "xt_w")
         xt_s = held([P, T], U8, "xt_s")
-        xo_w = held([P, T], U32, "xo_w")
+        xo_w = boards.tile([P, T], U32, name="xo_w", offset=2 * C, align_bytes=64)
         xo_s = held([P, T], U8, "xo_s")
         vs_w = sums.tile([P, V], U16, name="vs_w", offset=4 * C - V, align_bytes=64)
         vs_s = sums.tile([P, V], U8, name="vs_s", offset=12 * C - V // 2, align_bytes=64)
@@ -74,7 +75,7 @@ def tile_picked_tokens_plain_bank_echo_store_plain_kernel(
         nc.sync.dma_start(out=w_raw[:].bitcast(I32), in_=w_words[0].rearrange("p n t -> p (n t)").bitcast(I32))
         nc.sync.dma_start(out=xt_w[:].bitcast(I32), in_=xt_words[0].bitcast(I32))
         nc.sync.dma_start(out=xo_w[:].bitcast(I32), in_=xo_words[0].rearrange("p n t -> p (n t)").bitcast(I32))
-        for q in range(4):
+        for q in (0, 2, 1, 3):
             load_rows(nc.sync, xo_s, xo_scales, q)
         nc.sync.dma_start(out=w2_raw[:].bitcast(I32), in_=w2_words[0].bitcast(I32))
         nc.sync.dma_start(l3[:], offs3)
@@ -92,17 +93,17 @@ def tile_picked_tokens_plain_bank_echo_store_plain_kernel(
         w2_first = held([P, P], U16, "w2_first")
         w2_rest = held([P, PACK - 1, P], U16, "w2_rest")
         w2_d = [w2_first[:]] + [w2_rest[:, t, :] for t in range(PACK - 1)]
-        nc.scalar.copy(out=w_d[:].rearrange("p t m -> p m t"), in_=w_raw[:].rearrange("p (m t) -> p m t", t=PACK))
-        w2_columns = w2_raw[:].rearrange("p (m t) -> p m t", t=PACK)
-        nc.scalar.copy(out=w2_first[:], in_=w2_columns[:, :, 0])
-        nc.scalar.copy(out=w2_rest[:].rearrange("p t m -> p m t"), in_=w2_columns[:, :, 1:PACK])
+        nc.scalar.copy(out=w_d[:].rearrange("p t (c i) -> p c t i", i=4), in_=w_raw[:].rearrange("p (c i t) -> p c t i", i=4, t=PACK))
+        w2_by_tile = w2_raw[:].rearrange("p (m t) -> p t m", t=PACK)
+        nc.scalar.copy(out=w2_first[:], in_=w2_by_tile[:, 0, :])
+        nc.scalar.copy(out=w2_rest[:], in_=w2_by_tile[:, 1:PACK, :])
 
         for q in range(4):
             nc.vector.tensor_copy(out=xt_s[32 * q : 32 * q + 4, :].bitcast(I32), in_=xt_stage[:, q, :])
             nc.vector.tensor_copy(out=spread[32 * q : 32 * q + 4], in_=w_stage[:, :, q, :])
         s_all = held([P, PACK, 2 * P], U8, "s_all")
-        by_column = spread[:].rearrange("p m c -> p (m c)").bitcast(U8).rearrange("p (c t) -> p c t", t=PACK)
-        nc.vector.tensor_copy(out=s_all[:].rearrange("p t c -> p c t"), in_=by_column)
+        by_column = spread[:].rearrange("p m c -> p (m c)").bitcast(U8).rearrange("p (c t) -> p t c", t=PACK)
+        nc.vector.tensor_copy(out=s_all[:], in_=by_column)
         s_d = [s_all[:, t, :] for t in range(PACK)]
 
         xg_w = [held([P, H], U16, "xg_w0"), reused.tile([P, H], U16, name="xg_w1", offset=0, align_bytes=64)]
@@ -145,9 +146,6 @@ def tile_picked_tokens_plain_bank_echo_store_plain_kernel(
                 product(acc[:, t - SPLIT, h, :], t, h)
         nc.vector.tensor_copy(out=whole[:].rearrange("p t j -> p (t j)"), in_=acc[:].rearrange("p t h j -> p (t h j)"))
 
-        pv = [held([P, C], F32, "pv%d" % t, tag=tag) for t, tag in enumerate(("xt_w", "xt_s", "xo_s", "xo_w"))]
-        for t in range(PACK):
-            nc.gpsimd.memset(pv[t][:], 0.0)
         h1 = [held([P, S], F32, "h1_%d" % t) for t in range(PACK)]
 
         def put_a(t, src, first, count):
@@ -167,6 +165,10 @@ def tile_picked_tokens_plain_bank_echo_store_plain_kernel(
         for t in range(SPLIT, PACK):
             put_a(t, whole[:, t - SPLIT, :], 0, J)
 
+        pv = [boards.tile([P, C], F32, name="pv%d" % t, offset=4 * C * t, align_bytes=64) for t in range(PACK - 1)]
+        pv.append(held([P, C], F32, "pv3", tag="early0"))
+        for t in range(PACK):
+            nc.gpsimd.memset(pv[t][:], 0.0)
         vg_w = held([P, N], U16, "vg_w", tag="early2")
         vg_s = held([P, N], U8, "vg_s", tag="late")
         nc.vector.tensor_copy(out=vg_s[:], in_=vs_s[:].indirect(l7[:]))

from contextlib import ExitStack

import concourse.mybir as mybir

F32 = mybir.dt.float32
BF16 = mybir.dt.bfloat16
I32 = mybir.dt.int32
U32 = mybir.dt.uint32
U16 = mybir.dt.uint16
U8 = mybir.dt.uint8
FP8X4 = mybir.dt.float8_e4m3fn_x4
FP4X4 = mybir.dt.float4_e2m1fn_x4
COPY = mybir.ActivationFunctionType.Copy
ADD = mybir.AluOpType.add

P = 128
PACK = 4
J, R, T, C, O, S, N, V = 256, 512, 1024, 512, 128, 128, 256, 1024
H = J // 2
SPLIT = 3
FLOPS = 2 * (512 * R * J + 512 * R * J + R * N * O)


def tile_picked_tokens_plain_bank_echo_store_plain_kernel(
    tc, xt_words, xt_scales, w_words, w_scales, xo_words, xo_scales, w2_words, w2_scales,
    sa, sb, vs_words, vs_scales, offs, offs2, offs3, offs4, offs5, offs6, offs7, out,
):
    nc = tc.nc
    with ExitStack() as ctx:
        lists = ctx.enter_context(tc.tile_pool(name="lists", bufs=1))
        sbuf = ctx.enter_context(tc.tile_pool(name="sbuf", bufs=1))
        reused = ctx.enter_context(tc.tile_pool(name="reused", bufs=1))
        sums = ctx.enter_context(tc.tile_pool(name="sums", bufs=1))
        boards = ctx.enter_context(tc.tile_pool(name="boards", bufs=1))
        psum = ctx.enter_context(tc.psum_pool(name="psum", bufs=1))

        def held(shape, dtype, name, tag=None):
            return sbuf.tile(shape, dtype, name=name, tag=tag or name, align_bytes=64)

        def list_tile(src, name):
            return lists.tile(list(src.shape), U16, name=name)

        def load_rows(queue, window, scales, q):
            queue.dma_start(out=window[32 * q : 32 * q + 4, :].bitcast(I32), in_=scales[0, 4 * q : 4 * q + 4, :].bitcast(I32))

        l1, l2, l3, l4, l5, l6, l7 = [
            list_tile(src, "list%d" % i) for i, src in enumerate((offs, offs2, offs3, offs4, offs5, offs6, offs7))
        ]
        xt_w = held([P, T], U16, "xt_w")
        xt_s = held([P, T], U8, "xt_s")
        xo_w = boards.tile([P, T], U32, name="xo_w", offset=2 * C, align_bytes=64)
        xo_s = held([P, T], U8, "xo_s")
        vs_w = sums.tile([P, V], U16, name="vs_w", offset=4 * C - V, align_bytes=64)
        vs_s = sums.tile([P, V], U8, name="vs_s", offset=12 * C - V // 2, align_bytes=64)
        w_raw = held([P, R], U32, "w_raw")
        w2_raw = reused.tile([P, R], U16, name="w2_raw", offset=0, align_bytes=64)
        xt_stage = held([4, 4, T // 4], I32, "xt_stage")
        w_stage = held([4, 2, 4, R // 4], I32, "w_stage")
        spread = held([P, 2, R // 4], I32, "spread")
        sa_t = held([P, PACK], F32, "sa_t")
        sb_t = held([P, PACK], F32, "sb_t")
        pw = [held([P, C], F32, "pw%d" % t) for t in range(PACK)]

        for win in (xo_s, xt_s):
            nc.vector.memset(win[:].bitcast(I32), 0)
        nc.vector.memset(spread[:], 0)
        for t in range(PACK):
            (nc.vector if t < 3 else nc.gpsimd).memset(pw[t][:], 0.0)
        nc.gpsimd.memset(vs_s[:].bitcast(I32), 0)

        for stage, scales in ((xt_stage[:], xt_scales), (w_stage[:, 0], w_scales), (w_stage[:, 1], w2_scales)):
            nc.sync.dma_start(out=stage, in_=scales[0].bitcast(I32).rearrange("(q i) c -> i q c", i=4))
        nc.sync.dma_start(l1[:], offs)
        nc.sync.dma_start(l2[:], offs2)
        nc.sync.dma_start(out=w_raw[:].bitcast(I32), in_=w_words[0].rearrange("p n t -> p (n t)").bitcast(I32))
        nc.sync.dma_start(out=xt_w[:].bitcast(I32), in_=xt_words[0].bitcast(I32))
        nc.sync.dma_start(out=xo_w[:].bitcast(I32), in_=xo_words[0].rearrange("p n t -> p (n t)").bitcast(I32))
        for q in (0, 2, 1, 3):
            load_rows(nc.sync, xo_s, xo_scales, q)
        nc.sync.dma_start(out=w2_raw[:].bitcast(I32), in_=w2_words[0].bitcast(I32))
        nc.sync.dma_start(l3[:], offs3)
        nc.sync.dma_start(l4[:], offs4)
        nc.sync.dma_start(out=sa_t[:], in_=sa.rearrange("(p t) o -> p (t o)", t=PACK))
        nc.sync.dma_start(l5[:], offs5)
        nc.sync.dma_start(l7[:], offs7)
        nc.sync.dma_start(out=vs_w[:].bitcast(I32), in_=vs_words[0].bitcast(I32))
        for q in range(4):
            load_rows(nc.sync, vs_s, vs_scales, q)
        nc.sync.dma_start(l6[:], offs6)
        nc.sync.dma_start(out=sb_t[:], in_=sb.rearrange("(p t) o -> p (t o)", t=PACK))

        w_d = held([P, PACK, P], U32, "w_d")
        w2_first = held([P, P], U16, "w2_first")
        w2_rest = held([P, PACK - 1, P], U16, "w2_rest")
        w2_d = [w2_first[:]] + [w2_rest[:, t, :] for t in range(PACK - 1)]
        nc.scalar.copy(out=w_d[:].rearrange("p t (c i) -> p c t i", i=4), in_=w_raw[:].rearrange("p (c i t) -> p c t i", i=4, t=PACK))
        w2_by_tile = w2_raw[:].rearrange("p (m t) -> p t m", t=PACK)
        nc.scalar.copy(out=w2_first[:], in_=w2_by_tile[:, 0, :])
        nc.scalar.copy(out=w2_rest[:], in_=w2_by_tile[:, 1:PACK, :])

        for q in range(4):
            nc.vector.tensor_copy(out=xt_s[32 * q : 32 * q + 4, :].bitcast(I32), in_=xt_stage[:, q, :])
            nc.vector.tensor_copy(out=spread[32 * q : 32 * q + 4], in_=w_stage[:, :, q, :])
        s_all = held([P, PACK, 2 * P], U8, "s_all")
        by_column = spread[:].rearrange("p m c -> p (m c)").bitcast(U8).rearrange("p (c t) -> p t c", t=PACK)
        nc.vector.tensor_copy(out=s_all[:], in_=by_column)
        s_d = [s_all[:, t, :] for t in range(PACK)]

        xg_w = [held([P, H], U16, "xg_w0"), reused.tile([P, H], U16, name="xg_w1", offset=0, align_bytes=64)]
        xg_s = [held([P, H], U8, "xg_s0"), reused.tile([P, H], U8, name="xg_s1", offset=2 * H, align_bytes=64)]
        og_s = [held([P, H], U8, "og_s0"), reused.tile([P, H], U8, name="og_s1", offset=3 * H, align_bytes=64)]
        og_w = [held([P, H], U32, "og_w0"), reused.tile([P, H], U32, name="og_w1", offset=4 * H, align_bytes=64)]

        def gather_half(h):
            cols = slice(h * H // 16, (h + 1) * H // 16)
            nc.vector.tensor_copy(out=xg_w[h][:], in_=xt_w[:].indirect(l1[:, cols]))
            nc.vector.tensor_copy(out=xg_s[h][:], in_=xt_s[:].indirect(l1[:, cols]))
            nc.vector.tensor_copy(out=og_s[h][:], in_=xo_s[:].indirect(l2[:, cols]))
            nc.vector.tensor_copy(out=og_w[h][:], in_=xo_w[:].indirect(l2[:, cols]))

        def product(acc, t, h):
            nc.tensor.matmul_mx(out=acc, lhsT=w_d[:, t, :].bitcast(FP8X4), lhsT_scale=s_d[t][:, 0:P],
                                rhs=xg_w[h][:].bitcast(FP4X4), rhs_scale=xg_s[h][:], start=True, stop=False)
            nc.tensor.matmul_mx(out=acc, lhsT=w2_d[t].bitcast(FP4X4), lhsT_scale=s_d[t][:, P : 2 * P],
                                rhs=og_w[h][:].bitcast(FP8X4), rhs_scale=og_s[h][:], start=False, stop=True)

        gather_half(0)
        early = [held([P, H], F32, "early%d" % t) for t in range(SPLIT)]
        for t in range(SPLIT):
            acc = psum.tile([P, H], F32, name="acc_early%d" % t)
            product(acc[:], t, 0)
            if t == 0:
                nc.scalar.activation(out=early[t][:], in_=acc[:], func=COPY)
            else:
                nc.vector.tensor_copy(out=early[t][:], in_=acc[:])
        gather_half(1)
        late = held([P, SPLIT, H], F32, "late")
        acc = psum.tile([P, SPLIT, H], F32, name="acc_late")
        for t in range(SPLIT):
            product(acc[:, t, :], t, 1)
        nc.vector.tensor_copy(out=late[:], in_=acc[:])
        whole = held([P, PACK - SPLIT, J], F32, "whole")
        acc = psum.tile([P, PACK - SPLIT, 2, H], F32, name="acc_whole")
        for h in range(2):
            for t in range(SPLIT, PACK):
                product(acc[:, t - SPLIT, h, :], t, h)
        nc.vector.tensor_copy(out=whole[:].rearrange("p t j -> p (t j)"), in_=acc[:].rearrange("p t h j -> p (t h j)"))

        h1 = [held([P, S], F32, "h1_%d" % t) for t in range(PACK)]

        def put_a(t, src, first, count):
            nc.scalar.activation(out=pw[t][:].indirect(l3[:, first // 16 : (first + count) // 16]), in_=src, func=COPY)

        def take(t):
            nc.scalar.activation(out=h1[t][:], in_=pw[t][:].indirect(l4[:]), func=COPY, scale=sa_t[:, t : t + 1])

        def put_echo(t):
            nc.scalar.activation(out=pv[t][:].indirect(l5[:]), in_=h1[t][:], func=COPY)
            nc.vector.tensor_tensor(out=pg[t][:], in0=pw[t][:], in1=pv[t][:], op=ADD)

        for t in range(SPLIT):
            put_a(t, early[t][:], 0, H)
        for t in range(SPLIT):
            put_a(t, late[:, t, :], H, H)
        for t in range(SPLIT, PACK):
            put_a(t, whole[:, t - SPLIT, :], 0, J)

        pv = [boards.tile([P, C], F32, name="pv%d" % t, offset=4 * C * t, align_bytes=64) for t in range(PACK - 1)]
        pv.append(held([P, C], F32, "pv3", tag="early0"))
        for t in range(PACK):
            nc.gpsimd.memset(pv[t][:], 0.0)
        vg_w = held([P, N], U16, "vg_w", tag="early2")
        vg_s = held([P, N], U8, "vg_s", tag="late")
        nc.vector.tensor_copy(out=vg_s[:], in_=vs_s[:].indirect(l7[:]))
        nc.vector.tensor_copy(out=vg_w[:], in_=vs_w[:].indirect(l7[:]))
        pg = [sums.tile([P, C], F32, name="pg%d" % t, offset=4 * C * t, align_bytes=64) for t in range(PACK)]
        for t in range(PACK):
            take(t)
        for t in range(PACK):
            put_echo(t)

        hid = held([P, PACK, O], BF16, "hid", tag="h1_3")
        for t in range(PACK):
            nc.scalar.activation(out=hid[:, t, :], in_=pg[t][:].indirect(l6[:]), func=COPY, scale=sb_t[:, t : t + 1])

        woven = [held([P, O // 2, PACK], BF16, "woven%d" % u) for u in range(2)]
        hq_w = held([P, O], U32, "hq_w")
        hq_s = held([P, O], U8, "hq_s")
        for u in range(2):
            nc.vector.tensor_copy(out=woven[u][:], in_=hid[:, :, u * 64 : (u + 1) * 64].rearrange("p t o -> p o t"))
        for u in range(2):
            nc.vector.quantize_mx(out=hq_w[:, u * 64 : (u + 1) * 64].bitcast(FP8X4), scales=hq_s[:, u * 64 : (u + 1) * 64],
                                  in_=woven[u][:].rearrange("p o t -> p (o t)"))
        for u in range(2):
            y = psum.tile([P, O], F32, name="y%d" % u)
            nc.tensor.matmul_mx(out=y[:], lhsT=vg_w[:, u * P : (u + 1) * P].bitcast(FP4X4), lhsT_scale=vg_s[:, u * P : (u + 1) * P],
                                rhs=hq_w[:].bitcast(FP8X4), rhs_scale=hq_s[:], start=True, stop=True)
            res = held([P, O], F32, "res%d" % u)
            if u == 0:
                nc.vector.tensor_copy(out=res[:], in_=y[:])
                nc.sync.dma_start(out=out[u * P : (u + 1) * P, :], in_=res[:])
            else:
                nc.scalar.activation(out=res[:], in_=y[:], func=COPY)
                nc.scalar.dma_start(out=out[u * P : (u + 1) * P, :], in_=res[:])
